import numpy as np
import ml_dtypes


def mxq(x, axis, fmt="e4m3"):
    dtype, down = {"e4m3": (ml_dtypes.float8_e4m3fn, 7), "e5m2": (ml_dtypes.float8_e5m2, 14)}[fmt]
    v = np.moveaxis(np.asarray(x, np.float32).astype(ml_dtypes.bfloat16).astype(np.float64), axis, -1)
    blocks = v.reshape(v.shape[:-1] + (-1, 32))
    amax = np.abs(blocks).max(-1, keepdims=True)
    byte = np.maximum(np.where(amax > 0, np.frexp(amax)[1] - 1 + 127, 0) - down, 1)
    scale = np.exp2(byte - 127.0)
    codes = (blocks / scale).astype(np.float32).astype(dtype).astype(np.float64)
    return np.moveaxis((codes * scale).reshape(v.shape), -1, axis)


WIDE = False


def mx_kscale(k):
    if not WIDE:
        return np.ones(k)
    levels = np.array([10, -10, 5, -5, 0])
    if k % 512:
        return np.exp2(np.random.permutation(np.resize(levels, k // 32))).repeat(32)
    a = np.empty((k // 512, 16))
    for p in range(k // 512):
        a[p, :8] = np.random.permutation(np.resize(levels, 8))
        for g in range(8):
            far = levels[np.abs(levels - a[p, g]) >= 10]
            a[p, g + 8] = far[np.random.randint(len(far))]
    return np.exp2(a.ravel()).repeat(32)


def f64(x):
    return np.asarray(x).astype(np.float64)


def striped(idx):
    return np.tile(idx.reshape(-1, 16).T, (8, 1)).astype(np.uint16)


def unstriped(offs):
    return offs[:16].T.reshape(-1).astype(np.int64)


def striped8(idx):
    return np.concatenate([x.reshape(-1, 16).T for x in idx]).astype(np.uint16)


def runs(offs, k):
    lists = np.stack([offs[16 * r : 16 * r + 16].T.reshape(-1) for r in range(8)]).astype(np.int64)
    return lists[np.arange(k) % 512 // 64]


def pack_weight(w):
    k, n = w.shape
    w = f64(np.asarray(w, np.float32).astype(ml_dtypes.bfloat16)).reshape(k // 32, 32, n)
    amax = np.abs(w).max(1)
    byte = np.clip(np.where(amax > 0, np.frexp(amax)[1] - 1 + 127 - 7, 1), 1, 254)
    scaled = (w * np.exp2(127.0 - byte)[:, None, :]).reshape(k, n).astype(np.float32)
    words = np.ascontiguousarray(scaled.reshape(k // 512, 128, 4, n).transpose(0, 1, 3, 2)).astype(ml_dtypes.float8_e4m3fn).view(np.uint8)
    return words, np.ascontiguousarray(byte.astype(np.uint8).reshape(k // 512, 16, n))


def unpack_weight(words, scales):
    g, p, n, _ = words.shape
    vals = np.ascontiguousarray(words).view(ml_dtypes.float8_e4m3fn).astype(np.float64) * np.repeat(np.exp2(scales.astype(np.float64) - 127.0), 8, axis=1)[..., None]
    return vals.transpose(0, 1, 3, 2).reshape(g * 512, n)


K, T, S, G, H = 512, 1024, 512, 2048, 512


def setup_inputs():
    n = np.random.standard_normal
    s = mx_kscale(K)[:, None]
    packed_xT = pack_weight(n((K, T)) * s)
    packed_dT = pack_weight(n((K, G)) / s)
    return {
        "x_words": packed_xT[0],
        "x_scales": packed_xT[1],
        "d_words": packed_dT[0],
        "d_scales": packed_dT[1],
        "gs": (np.random.uniform(0.5, 1.5, (K, 1)) * s).astype(np.float32),
        "offs": striped(np.random.permutation(T)[:S]),
        "k1": striped8(np.random.randint(0, G, (8, H))),
        "n1": striped(np.random.permutation(S)),
        "n2": striped(np.random.permutation(S)),
        "n3": striped(np.random.permutation(S)),
        "k2": striped8(np.random.randint(0, G, (8, H))),
        "n4": striped(np.random.permutation(S)),
        "n5": striped(np.random.permutation(S)),
    }


def reference(x_words, x_scales, d_words, d_scales, gs, offs, k1, n1, n2, n3, k2, n4, n5):
    d_k2 = unpack_weight(d_words, d_scales)[np.arange(K)[:, None], runs(k2, K)]
    d_k1 = unpack_weight(d_words, d_scales)[np.arange(K)[:, None], runs(k1, K)]
    xq = unpack_weight(x_words, x_scales)[:, unstriped(offs)]
    h = 0.0625 * (d_k1.T @ xq)
    z = f64(gs) * (h + h[:, unstriped(n1)] - (np.maximum(h[:, unstriped(n2)], h[:, unstriped(n3)])))
    h2 = 0.0625 * ((d_k2.T @ mxq(z, 0, "e4m3")))
    st = np.maximum(h2, h2[:, unstriped(n4)])
    return st[:, unstriped(n5)] - (0.5 * h2)

@@ -1,0 +1,210 @@
+from contextlib import ExitStack
+
+import concourse.mybir as mybir
+from concourse.masks import make_identity
+
+F32 = mybir.dt.float32
+BF16 = mybir.dt.bfloat16
+I32 = mybir.dt.int32
+U32 = mybir.dt.uint32
+U16 = mybir.dt.uint16
+U8 = mybir.dt.uint8
+FP8X4 = mybir.dt.float8_e4m3fn_x4
+ALU = mybir.AluOpType
+COPY = mybir.ActivationFunctionType.Copy
+
+P = 128
+K, T, S, G, H = 512, 1024, 512, 2048, 512
+TILES = H // P
+BLOCKS = S // P
+HALF = 256
+SIXTEENTH = 0.0625
+CHUNKS = ((0, 256), (256, 384), (384, 512))
+HALVES = ((0, HALF), (HALF, 2 * HALF))
+
+FLOPS = 2 * (2 * K * H * S)
+
+
+def tile_picked_codetrimhopb_none_p_kernel(
+    tc, x_words, x_scales, d_words, d_scales, gs, offs, k1, n1, n2, n3, k2, n4, n5, out
+):
+    nc = tc.nc
+    with ExitStack() as ctx:
+        held = ctx.enter_context(tc.tile_pool(name="held", bufs=1))
+        ring = ctx.enter_context(tc.tile_pool(name="ring", bufs=6))
+        psum = ctx.enter_context(tc.psum_pool(name="psum", bufs=1))
+
+        def load_list(name, source):
+            tile = held.tile([P, S // 16], U16, name=name)
+            nc.sync.dma_start(tile[:], source)
+            return tile
+
+        def entries(tile, lo, hi):
+            return tile[:, lo // 16 : hi // 16]
+
+        d_bytes = held.tile([P, G], U8, name="d_bytes")
+        x_bytes = held.tile([P, T], U8, name="x_bytes")
+        nc.vector.memset(d_bytes[:].bitcast(I32), 0)
+        nc.vector.memset(x_bytes[:].bitcast(I32), 0)
+
+        k1_t = load_list("k1_t", k1)
+        offs_t = load_list("offs_t", offs)
+        nc.sync.dma_start(d_bytes[0:P:8, :].bitcast(I32), d_scales[0].bitcast(I32))
+        nc.sync.dma_start(x_bytes[0:P:8, :].bitcast(I32), x_scales[0].bitcast(I32))
+        x_table = held.tile([P, T], U32, name="x_table")
+        nc.sync.dma_start(x_table[:].bitcast(I32), x_words[0].rearrange("p n t -> p (n t)").bitcast(I32))
+        n3_t = load_list("n3_t", n3)
+        n1_t = load_list("n1_t", n1)
+        d_table = held.tile([P, G], U32, name="d_table")
+        nc.sync.dma_start(d_table[:].bitcast(I32), d_words[0].rearrange("p n t -> p (n t)").bitcast(I32))
+        k2_t = load_list("k2_t", k2)
+        n2_t = load_list("n2_t", n2)
+        n4_t = load_list("n4_t", n4)
+        n5_t = load_list("n5_t", n5)
+        gs_t = held.tile([P, 4], F32, name="gs_t")
+        nc.gpsimd.dma_start(gs_t[:], gs.rearrange("(p t) o -> p (t o)", t=4))
+
+        identity = held.tile([P, P], F32, name="identity")
+        make_identity(nc, identity[:])
+
+        def place_rows(name, picked, width):
+            planes = held.tile([P, width], U8, name=name, align_bytes=64)
+            nc.vector.tensor_copy(planes[:].bitcast(I32), picked[:].bitcast(I32))
+            for r in range(1, 4):
+                nc.sync.dma_start(planes[r:P:32, :].bitcast(I32), picked[8 * r : P : 32, :].bitcast(I32))
+            return planes
+
+        early = held.tile([P, H + S], U8, name="early", tag="picked_bytes")
+        nc.vector.tensor_copy(early[:, :H], d_bytes[:].indirect(k1_t[:]))
+        nc.vector.tensor_copy(early[:, H:], x_bytes[:].indirect(offs_t[:]))
+        early_planes = place_rows("early_planes", early, H + S)
+        x_plane = early_planes[:, H:]
+        x_codes = held.tile([P, S], U32, name="x_codes", align_bytes=64)
+        nc.vector.tensor_copy(x_codes[:], x_table[:].indirect(offs_t[:]))
+
+        gs_bank = psum.tile([P, 4, P], F32, name="gs_bank", tag="turn")
+        for t in range(4):
+            nc.tensor.transpose(gs_bank[:, t, :], gs_t[:, t : t + 1].to_broadcast([P, P]), identity[:])
+        gs_row = held.tile([P, P, 4], F32, name="gs_row")
+        nc.scalar.activation(gs_row[:], gs_bank[:].rearrange("p t n -> p n t"), COPY)
+
+        h = []
+
+        def first_product(i):
+            lo, hi = HALVES[i]
+            codes = held.tile([P, HALF], U32, name="w1_codes%d" % i, align_bytes=64)
+            nc.vector.tensor_copy(codes[:], d_table[:].indirect(entries(k1_t, lo, hi)))
+            for t in (2 * i, 2 * i + 1):
+                cols = slice(P * t - lo, P * (t + 1) - lo)
+                bank = psum.tile([P, S], F32, name="h_bank%d" % t, tag="rows%d" % t)
+                nc.tensor.matmul_mx(
+                    out=bank[:],
+                    lhsT=codes[:, cols].bitcast(FP8X4),
+                    lhsT_scale=early_planes[:, P * t : P * (t + 1)],
+                    rhs=x_codes[:].bitcast(FP8X4),
+                    rhs_scale=x_plane,
+                    start=True,
+                    stop=True,
+                )
+                row = held.tile([P, S], F32, name="h%d" % t, tag="window%d" % t)
+                nc.scalar.activation(row[:], bank[:], COPY, scale=SIXTEENTH)
+                h.append(row)
+
+        first_product(0)
+        first_product(1)
+        late = held.tile([P, H], U8, name="late", tag="picked_bytes")
+        nc.vector.tensor_copy(late[:], d_bytes[:].indirect(k2_t[:]))
+        w2_plane = place_rows("w2_plane", late, H)
+        w2_codes = held.tile([P, H], U32, name="w2_codes", align_bytes=64)
+        nc.vector.tensor_copy(w2_codes[:], d_table[:].indirect(k2_t[:]))
+
+        h2_banks = [psum.tile([P, S], F32, name="h2_bank%d" % t, tag="rows%d" % t) for t in range(TILES)]
+
+        def finish_block(b, sums):
+            z_turned = held.tile([P, H], BF16, name="z_turned%d" % b)
+            nc.vector.tensor_tensor(z_turned[:], sums[:], gs_row[:].rearrange("p n t -> p (n t)"), ALU.mult)
+            pairs = z_turned[:].bitcast(F32)
+            back = psum.tile([P, 2, P], F32, name="back%d" % b, tag="turn")
+            for u in range(2):
+                nc.tensor.transpose(back[:, u, :], pairs[:, u : H // 2 : 2], identity[:])
+            z_grouped = held.tile([P, P, 2], F32, name="z_grouped%d" % b, align_bytes=64)
+            nc.vector.tensor_copy(z_grouped[:], back[:].rearrange("p u r -> p r u"))
+            z_codes = held.tile([P, P], U32, name="z_codes%d" % b, align_bytes=64)
+            z_plane = held.tile([P, P], U8, name="z_plane%d" % b, align_bytes=64)
+            nc.vector.quantize_mx(
+                out=z_codes[:].bitcast(FP8X4),
+                scales=z_plane[:],
+                in_=z_grouped[:].rearrange("p r u -> p (r u)").bitcast(BF16),
+            )
+            for t in range(TILES):
+                nc.tensor.matmul_mx(
+                    out=h2_banks[t][:, P * b : P * (b + 1)],
+                    lhsT=w2_codes[:, P * t : P * (t + 1)].bitcast(FP8X4),
+                    lhsT_scale=w2_plane[:, P * t : P * (t + 1)],
+                    rhs=z_codes[:].bitcast(FP8X4),
+                    rhs_scale=z_plane[:],
+                    start=True,
+                    stop=True,
+                )
+
+        h2 = []
+        last = S - P
+        for c, (lo, hi) in enumerate(CHUNKS):
+            blocks = range(lo // P, hi // P)
+            sums = {b: psum.tile([P, H], F32, name="sums%d" % b, tag="sums%d" % (b % 3)) for b in blocks}
+            for t in range(TILES):
+                at1 = held.tile([P, hi - lo], F32, name="at1_%d_%d" % (c, t))
+                at2 = ring.tile([P, hi - lo], F32, name="at2_%d_%d" % (c, t), tag="at2")
+                minus3 = held.tile([P, hi - lo], F32, name="minus3_%d_%d" % (c, t))
+                least = held.tile([P, hi - lo], F32, name="least_%d_%d" % (c, t))
+                nc.scalar.activation(minus3[:], h[t][:].indirect(entries(n3_t, lo, hi)), COPY, scale=-1.0)
+                nc.scalar.activation(at1[:], h[t][:].indirect(entries(n1_t, lo, hi)), COPY)
+                nc.vector.tensor_copy(at2[:], h[t][:].indirect(entries(n2_t, lo, hi)))
+                nc.vector.scalar_tensor_tensor(least[:], at2[:], -1.0, minus3[:], ALU.mult, ALU.min)
+                for b in blocks:
+                    terms = (h[t][:, P * b : P * (b + 1)], least[:, P * b - lo : P * (b + 1) - lo], at1[:, P * b - lo : P * (b + 1) - lo])
+                    for i, term in enumerate(terms):
+                        nc.tensor.matmul(
+                            sums[b][:, P * t : P * (t + 1)], term, identity[:], start=(i == 0), stop=(i == 2), is_transpose=True
+                        )
+            for b in blocks:
+                if b == BLOCKS - 1:
+                    for t in range(TILES):
+                        row = held.tile([P, S], F32, name="h2_%d" % t, tag="window%d" % t)
+                        nc.scalar.activation(row[:, :last], h2_banks[t][:, :last], COPY, scale=SIXTEENTH)
+                        h2.append(row)
+                finish_block(b, sums[b])
+        for t in range(TILES):
+            if t % 2:
+                nc.scalar.activation(h2[t][:, last:], h2_banks[t][:, last:], COPY, scale=SIXTEENTH)
+            else:
+                nc.vector.tensor_scalar(h2[t][:, last:], h2_banks[t][:, last:], SIXTEENTH, None, ALU.mult)
+
+        st = [held.tile([P, S], F32, name="st%d" % t) for t in range(TILES)]
+        at4 = [held.tile([P, S], F32, name="at4_%d" % t) for t in range(TILES)]
+
+        def larger(t):
+            for lo, hi in HALVES:
+                picked = h2[t][:].indirect(entries(n4_t, lo, hi))
+                if t % 2:
+                    nc.scalar.activation(at4[t][:, lo:hi], picked, COPY)
+                else:
+                    nc.vector.tensor_copy(at4[t][:, lo:hi], picked)
+            nc.vector.tensor_tensor(st[t][:], h2[t][:], at4[t][:], ALU.max)
+
+        def result(t):
+            for i, (lo, hi) in enumerate(HALVES):
+                at5 = held.tile([P, hi - lo], F32, name="at5_%d_%d" % (t, i))
+                nc.scalar.activation(at5[:], st[t][:].indirect(entries(n5_t, lo, hi)), COPY)
+                piece = held.tile([P, hi - lo], F32, name="piece_%d_%d" % (t, i))
+                nc.vector.scalar_tensor_tensor(piece[:], h2[t][:, lo:hi], -0.5, at5[:], ALU.mult, ALU.add)
+                nc.sync.dma_start(out[P * t : P * (t + 1), lo:hi], piece[:])
+
+        larger(0)
+        larger(1)
+        result(0)
+        larger(2)
+        larger(3)
+        result(1)
+        result(2)
+        result(3)

@@ -19,7 +19,7 @@ TILES = H // P
 BLOCKS = S // P
 HALF = 256
 SIXTEENTH = 0.0625
-CHUNKS = ((0, 256), (256, 384), (384, 512))
+CHUNKS = ((0, 384), (384, 512))
 HALVES = ((0, HALF), (HALF, 2 * HALF))
 
 FLOPS = 2 * (2 * K * H * S)
@@ -31,7 +31,7 @@ def tile_picked_codetrimhopb_none_p_kernel(
     nc = tc.nc
     with ExitStack() as ctx:
         held = ctx.enter_context(tc.tile_pool(name="held", bufs=1))
-        ring = ctx.enter_context(tc.tile_pool(name="ring", bufs=6))
+        ring = ctx.enter_context(tc.tile_pool(name="ring", bufs=4))
         psum = ctx.enter_context(tc.psum_pool(name="psum", bufs=1))
 
         def load_list(name, source):
@@ -55,34 +55,35 @@ def tile_picked_codetrimhopb_none_p_kernel(
         nc.sync.dma_start(x_table[:].bitcast(I32), x_words[0].rearrange("p n t -> p (n t)").bitcast(I32))
         n3_t = load_list("n3_t", n3)
         n1_t = load_list("n1_t", n1)
+        k2_t = load_list("k2_t", k2)
         d_table = held.tile([P, G], U32, name="d_table")
         nc.sync.dma_start(d_table[:].bitcast(I32), d_words[0].rearrange("p n t -> p (n t)").bitcast(I32))
-        k2_t = load_list("k2_t", k2)
         n2_t = load_list("n2_t", n2)
         n4_t = load_list("n4_t", n4)
         n5_t = load_list("n5_t", n5)
         gs_t = held.tile([P, 4], F32, name="gs_t")
         nc.gpsimd.dma_start(gs_t[:], gs.rearrange("(p t) o -> p (t o)", t=4))
 
+        early_planes = held.tile([P, H + S], U8, name="early_planes", align_bytes=64)
+        w2_plane = held.tile([P, H], U8, name="w2_plane", align_bytes=64)
+        nc.gpsimd.memset(early_planes[:].bitcast(I32), 0)
+        nc.gpsimd.memset(w2_plane[:].bitcast(I32), 0)
         identity = held.tile([P, P], F32, name="identity")
         make_identity(nc, identity[:])
 
-        def place_rows(name, picked, width):
-            planes = held.tile([P, width], U8, name=name, align_bytes=64)
-            nc.vector.tensor_copy(planes[:].bitcast(I32), picked[:].bitcast(I32))
-            for r in range(1, 4):
-                nc.sync.dma_start(planes[r:P:32, :].bitcast(I32), picked[8 * r : P : 32, :].bitcast(I32))
-            return planes
+        def place_rows(planes, picked):
+            for q in range(4):
+                nc.sync.dma_start(planes[32 * q : 32 * q + 4, :].bitcast(I32), picked[32 * q : 32 * q + 32 : 8, :].bitcast(I32))
 
-        early = held.tile([P, H + S], U8, name="early", tag="picked_bytes")
+        early = held.tile([P, H + S], U8, name="early")
         nc.vector.tensor_copy(early[:, :H], d_bytes[:].indirect(k1_t[:]))
         nc.vector.tensor_copy(early[:, H:], x_bytes[:].indirect(offs_t[:]))
-        early_planes = place_rows("early_planes", early, H + S)
+        place_rows(early_planes, early)
         x_plane = early_planes[:, H:]
         x_codes = held.tile([P, S], U32, name="x_codes", align_bytes=64)
         nc.vector.tensor_copy(x_codes[:], x_table[:].indirect(offs_t[:]))
 
-        gs_bank = psum.tile([P, 4, P], F32, name="gs_bank", tag="turn")
+        gs_bank = psum.tile([P, 4, P], F32, name="gs_bank", tag="second0")
         for t in range(4):
             nc.tensor.transpose(gs_bank[:, t, :], gs_t[:, t : t + 1].to_broadcast([P, P]), identity[:])
         gs_row = held.tile([P, P, 4], F32, name="gs_row")
@@ -96,7 +97,7 @@ def tile_picked_codetrimhopb_none_p_kernel(
             nc.vector.tensor_copy(codes[:], d_table[:].indirect(entries(k1_t, lo, hi)))
             for t in (2 * i, 2 * i + 1):
                 cols = slice(P * t - lo, P * (t + 1) - lo)
-                bank = psum.tile([P, S], F32, name="h_bank%d" % t, tag="rows%d" % t)
+                bank = psum.tile([P, S], F32, name="h_bank%d" % t, tag="first%d" % t)
                 nc.tensor.matmul_mx(
                     out=bank[:],
                     lhsT=codes[:, cols].bitcast(FP8X4),
@@ -107,28 +108,36 @@ def tile_picked_codetrimhopb_none_p_kernel(
                     stop=True,
                 )
                 row = held.tile([P, S], F32, name="h%d" % t, tag="window%d" % t)
-                nc.scalar.activation(row[:], bank[:], COPY, scale=SIXTEENTH)
+                if t in (3,):
+                    nc.vector.tensor_scalar(row[:], bank[:], SIXTEENTH, None, ALU.mult)
+                else:
+                    nc.scalar.activation(row[:], bank[:], COPY, scale=SIXTEENTH)
                 h.append(row)
 
         first_product(0)
         first_product(1)
-        late = held.tile([P, H], U8, name="late", tag="picked_bytes")
+        late = held.tile([P, H], U8, name="late", tag="w1_codes0", align_bytes=64)
         nc.vector.tensor_copy(late[:], d_bytes[:].indirect(k2_t[:]))
-        w2_plane = place_rows("w2_plane", late, H)
+        place_rows(w2_plane, late)
         w2_codes = held.tile([P, H], U32, name="w2_codes", align_bytes=64)
         nc.vector.tensor_copy(w2_codes[:], d_table[:].indirect(k2_t[:]))
 
-        h2_banks = [psum.tile([P, S], F32, name="h2_bank%d" % t, tag="rows%d" % t) for t in range(TILES)]
+        h2_banks = [psum.tile([P, S], F32, name="h2_bank%d" % t, tag="second%d" % t) for t in range(TILES)]
+
+        quantised = {}
 
         def finish_block(b, sums):
             z_turned = held.tile([P, H], BF16, name="z_turned%d" % b)
             nc.vector.tensor_tensor(z_turned[:], sums[:], gs_row[:].rearrange("p n t -> p (n t)"), ALU.mult)
             pairs = z_turned[:].bitcast(F32)
-            back = psum.tile([P, 2, P], F32, name="back%d" % b, tag="turn")
+            back = psum.tile([P, 2, P], F32, name="back%d" % b, tag="first%d" % b)
             for u in range(2):
                 nc.tensor.transpose(back[:, u, :], pairs[:, u : H // 2 : 2], identity[:])
             z_grouped = held.tile([P, P, 2], F32, name="z_grouped%d" % b, align_bytes=64)
-            nc.vector.tensor_copy(z_grouped[:], back[:].rearrange("p u r -> p r u"))
+            if b in (0, 1, 2):
+                nc.scalar.copy(z_grouped[:], back[:].rearrange("p u r -> p r u"))
+            else:
+                nc.vector.tensor_copy(z_grouped[:], back[:].rearrange("p u r -> p r u"))
             z_codes = held.tile([P, P], U32, name="z_codes%d" % b, align_bytes=64)
             z_plane = held.tile([P, P], U8, name="z_plane%d" % b, align_bytes=64)
             nc.vector.quantize_mx(
@@ -136,6 +145,10 @@ def tile_picked_codetrimhopb_none_p_kernel(
                 scales=z_plane[:],
                 in_=z_grouped[:].rearrange("p r u -> p (r u)").bitcast(BF16),
             )
+            quantised[b] = (z_codes, z_plane)
+
+        def second_product(b):
+            z_codes, z_plane = quantised[b]
             for t in range(TILES):
                 nc.tensor.matmul_mx(
                     out=h2_banks[t][:, P * b : P * (b + 1)],
@@ -147,11 +160,19 @@ def tile_picked_codetrimhopb_none_p_kernel(
                     stop=True,
                 )
 
+        sums = [psum.tile([P, H], F32, name="sums%d" % b, tag="first%d" % b) for b in range(BLOCKS)]
+
+        def add_turned(b, t, term, start=False, stop=False):
+            nc.tensor.matmul(sums[b][:, P * t : P * (t + 1)], term, identity[:], start=start, stop=stop, is_transpose=True)
+
+        for b in range(BLOCKS):
+            for t in range(TILES):
+                add_turned(b, t, h[t][:, P * b : P * (b + 1)], start=(t == 0))
+
         h2 = []
         last = S - P
         for c, (lo, hi) in enumerate(CHUNKS):
             blocks = range(lo // P, hi // P)
-            sums = {b: psum.tile([P, H], F32, name="sums%d" % b, tag="sums%d" % (b % 3)) for b in blocks}
             for t in range(TILES):
                 at1 = held.tile([P, hi - lo], F32, name="at1_%d_%d" % (c, t))
                 at2 = ring.tile([P, hi - lo], F32, name="at2_%d_%d" % (c, t), tag="at2")
@@ -162,18 +183,20 @@ def tile_picked_codetrimhopb_none_p_kernel(
                 nc.vector.tensor_copy(at2[:], h[t][:].indirect(entries(n2_t, lo, hi)))
                 nc.vector.scalar_tensor_tensor(least[:], at2[:], -1.0, minus3[:], ALU.mult, ALU.min)
                 for b in blocks:
-                    terms = (h[t][:, P * b : P * (b + 1)], least[:, P * b - lo : P * (b + 1) - lo], at1[:, P * b - lo : P * (b + 1) - lo])
-                    for i, term in enumerate(terms):
-                        nc.tensor.matmul(
-                            sums[b][:, P * t : P * (t + 1)], term, identity[:], start=(i == 0), stop=(i == 2), is_transpose=True
-                        )
-            for b in blocks:
-                if b == BLOCKS - 1:
-                    for t in range(TILES):
-                        row = held.tile([P, S], F32, name="h2_%d" % t, tag="window%d" % t)
-                        nc.scalar.activation(row[:, :last], h2_banks[t][:, :last], COPY, scale=SIXTEENTH)
-                        h2.append(row)
-                finish_block(b, sums[b])
+                    add_turned(b, t, at1[:, P * b - lo : P * (b + 1) - lo])
+                for b in blocks:
+                    add_turned(b, t, least[:, P * b - lo : P * (b + 1) - lo], stop=(t == TILES - 1))
+            if hi < S:
+                for b in blocks:
+                    finish_block(b, sums[b])
+        finish_block(BLOCKS - 1, sums[BLOCKS - 1])
+        for b in range(BLOCKS - 1):
+            second_product(b)
+        for t in range(TILES):
+            row = held.tile([P, S], F32, name="h2_%d" % t, tag="window%d" % t)
+            nc.scalar.activation(row[:, :last], h2_banks[t][:, :last], COPY, scale=SIXTEENTH)
+            h2.append(row)
+        second_product(BLOCKS - 1)
         for t in range(TILES):
             if t % 2:
                 nc.scalar.activation(h2[t][:, last:], h2_banks[t][:, last:], COPY, scale=SIXTEENTH)
@@ -181,16 +204,16 @@ def tile_picked_codetrimhopb_none_p_kernel(
                 nc.vector.tensor_scalar(h2[t][:, last:], h2_banks[t][:, last:], SIXTEENTH, None, ALU.mult)
 
         st = [held.tile([P, S], F32, name="st%d" % t) for t in range(TILES)]
-        at4 = [held.tile([P, S], F32, name="at4_%d" % t) for t in range(TILES)]
 
         def larger(t):
+            at4 = held.tile([P, S], F32, name="at4_%d" % t, tag="at4_%d" % t if t % 2 else "at4_vector")
             for lo, hi in HALVES:
                 picked = h2[t][:].indirect(entries(n4_t, lo, hi))
                 if t % 2:
-                    nc.scalar.activation(at4[t][:, lo:hi], picked, COPY)
+                    nc.scalar.activation(at4[:, lo:hi], picked, COPY)
                 else:
-                    nc.vector.tensor_copy(at4[t][:, lo:hi], picked)
-            nc.vector.tensor_tensor(st[t][:], h2[t][:], at4[t][:], ALU.max)
+                    nc.vector.tensor_copy(at4[:, lo:hi], picked)
+            nc.vector.tensor_tensor(st[t][:], h2[t][:], at4[:], ALU.max)
 
         def result(t):
             for i, (lo, hi) in enumerate(HALVES):
@@ -200,11 +223,7 @@ def tile_picked_codetrimhopb_none_p_kernel(
                 nc.vector.scalar_tensor_tensor(piece[:], h2[t][:, lo:hi], -0.5, at5[:], ALU.mult, ALU.add)
                 nc.sync.dma_start(out[P * t : P * (t + 1), lo:hi], piece[:])
 
-        larger(0)
-        larger(1)
-        result(0)
-        larger(2)
-        larger(3)
-        result(1)
-        result(2)
-        result(3)
+        for t in (0, 1, 3, 2):
+            larger(t)
+        for t in (0, 1, 3, 2):
+            result(t)

@@ -22,6 +22,8 @@ SIXTEENTH = 0.0625
 CHUNKS = ((0, 384), (384, 512))
 HALVES = ((0, HALF), (HALF, 2 * HALF))
 
+ORDER = (1, 0, 3, 2)
+SPARE = 16
 FLOPS = 2 * (2 * K * H * S)
 
 
@@ -31,7 +33,7 @@ def tile_picked_codetrimhopb_none_p_kernel(
     nc = tc.nc
     with ExitStack() as ctx:
         held = ctx.enter_context(tc.tile_pool(name="held", bufs=1))
-        ring = ctx.enter_context(tc.tile_pool(name="ring", bufs=4))
+        ring = ctx.enter_context(tc.tile_pool(name="ring", bufs=2))
         psum = ctx.enter_context(tc.psum_pool(name="psum", bufs=1))
 
         def load_list(name, source):
@@ -44,13 +46,13 @@ def tile_picked_codetrimhopb_none_p_kernel(
 
         d_bytes = held.tile([P, G], U8, name="d_bytes")
         x_bytes = held.tile([P, T], U8, name="x_bytes")
-        nc.vector.memset(d_bytes[:].bitcast(I32), 0)
         nc.vector.memset(x_bytes[:].bitcast(I32), 0)
+        nc.vector.memset(d_bytes[:].bitcast(I32), 0)
 
-        k1_t = load_list("k1_t", k1)
         offs_t = load_list("offs_t", offs)
-        nc.sync.dma_start(d_bytes[0:P:8, :].bitcast(I32), d_scales[0].bitcast(I32))
+        k1_t = load_list("k1_t", k1)
         nc.sync.dma_start(x_bytes[0:P:8, :].bitcast(I32), x_scales[0].bitcast(I32))
+        nc.sync.dma_start(d_bytes[0:P:8, :].bitcast(I32), d_scales[0].bitcast(I32))
         x_table = held.tile([P, T], U32, name="x_table")
         nc.sync.dma_start(x_table[:].bitcast(I32), x_words[0].rearrange("p n t -> p (n t)").bitcast(I32))
         n3_t = load_list("n3_t", n3)
@@ -76,8 +78,8 @@ def tile_picked_codetrimhopb_none_p_kernel(
                 nc.sync.dma_start(planes[32 * q : 32 * q + 4, :].bitcast(I32), picked[32 * q : 32 * q + 32 : 8, :].bitcast(I32))
 
         early = held.tile([P, H + S], U8, name="early")
-        nc.vector.tensor_copy(early[:, :H], d_bytes[:].indirect(k1_t[:]))
         nc.vector.tensor_copy(early[:, H:], x_bytes[:].indirect(offs_t[:]))
+        nc.vector.tensor_copy(early[:, :H], d_bytes[:].indirect(k1_t[:]))
         place_rows(early_planes, early)
         x_plane = early_planes[:, H:]
         x_codes = held.tile([P, S], U32, name="x_codes", align_bytes=64)
@@ -108,7 +110,7 @@ def tile_picked_codetrimhopb_none_p_kernel(
                     stop=True,
                 )
                 row = held.tile([P, S], F32, name="h%d" % t, tag="window%d" % t)
-                if t in (3,):
+                if t in (2, 3):
                     nc.vector.tensor_scalar(row[:], bank[:], SIXTEENTH, None, ALU.mult)
                 else:
                     nc.scalar.activation(row[:], bank[:], COPY, scale=SIXTEENTH)
@@ -116,13 +118,19 @@ def tile_picked_codetrimhopb_none_p_kernel(
 
         first_product(0)
         first_product(1)
-        late = held.tile([P, H], U8, name="late", tag="w1_codes0", align_bytes=64)
+        late = held.tile([P, H], U8, name="late", tag="early")
         nc.vector.tensor_copy(late[:], d_bytes[:].indirect(k2_t[:]))
         place_rows(w2_plane, late)
         w2_codes = held.tile([P, H], U32, name="w2_codes", align_bytes=64)
         nc.vector.tensor_copy(w2_codes[:], d_table[:].indirect(k2_t[:]))
 
         h2_banks = [psum.tile([P, S], F32, name="h2_bank%d" % t, tag="second%d" % t) for t in range(TILES)]
+        later = {}
+
+        def h2_sums(t, lo, hi):
+            if lo < HALF:
+                return h2_banks[t][:, lo:hi]
+            return later[t][:, lo - HALF : hi - HALF]
 
         quantised = {}
 
@@ -149,9 +157,9 @@ def tile_picked_codetrimhopb_none_p_kernel(
 
         def second_product(b):
             z_codes, z_plane = quantised[b]
-            for t in range(TILES):
+            for t in ORDER:
                 nc.tensor.matmul_mx(
-                    out=h2_banks[t][:, P * b : P * (b + 1)],
+                    out=h2_sums(t, P * b, P * (b + 1)),
                     lhsT=w2_codes[:, P * t : P * (t + 1)].bitcast(FP8X4),
                     lhsT_scale=w2_plane[:, P * t : P * (t + 1)],
                     rhs=z_codes[:].bitcast(FP8X4),
@@ -169,8 +177,6 @@ def tile_picked_codetrimhopb_none_p_kernel(
             for t in range(TILES):
                 add_turned(b, t, h[t][:, P * b : P * (b + 1)], start=(t == 0))
 
-        h2 = []
-        last = S - P
         for c, (lo, hi) in enumerate(CHUNKS):
             blocks = range(lo // P, hi // P)
             for t in range(TILES):
@@ -184,46 +190,51 @@ def tile_picked_codetrimhopb_none_p_kernel(
                 nc.vector.scalar_tensor_tensor(least[:], at2[:], -1.0, minus3[:], ALU.mult, ALU.min)
                 for b in blocks:
                     add_turned(b, t, at1[:, P * b - lo : P * (b + 1) - lo])
-                for b in blocks:
                     add_turned(b, t, least[:, P * b - lo : P * (b + 1) - lo], stop=(t == TILES - 1))
-            if hi < S:
-                for b in blocks:
-                    finish_block(b, sums[b])
-        finish_block(BLOCKS - 1, sums[BLOCKS - 1])
-        for b in range(BLOCKS - 1):
-            second_product(b)
-        for t in range(TILES):
-            row = held.tile([P, S], F32, name="h2_%d" % t, tag="window%d" % t)
-            nc.scalar.activation(row[:, :last], h2_banks[t][:, :last], COPY, scale=SIXTEENTH)
-            h2.append(row)
-        second_product(BLOCKS - 1)
-        for t in range(TILES):
-            if t % 2:
-                nc.scalar.activation(h2[t][:, last:], h2_banks[t][:, last:], COPY, scale=SIXTEENTH)
-            else:
-                nc.vector.tensor_scalar(h2[t][:, last:], h2_banks[t][:, last:], SIXTEENTH, None, ALU.mult)
+        for b in range(BLOCKS):
+            finish_block(b, sums[b])
+        h2 = [held.tile([P, S + SPARE * (t % 2)], F32, name="h2_%d" % t, tag="window%d" % t) for t in range(TILES)]
+        for t in (1, 3):
+            nc.gpsimd.memset(h2[t][:, S:], 0.0)
+        scalar_bank = psum.tile([P, HALF], F32, name="later_scalar", tag="first0")
+        vector_bank = psum.tile([P, 2, HALF], F32, name="later_vector", tag="first1")
+        other_bank = psum.tile([P, HALF], F32, name="later_other", tag="first2")
+        later[1] = scalar_bank
+        later[3] = vector_bank[:, 0, :]
+        later[0] = vector_bank[:, 1, :]
+        later[2] = other_bank
+        for lo, hi in HALVES:
+            for b in range(lo // P, hi // P):
+                second_product(b)
+            for t in ORDER:
+                if hi == S and t != 1:
+                    nc.vector.tensor_scalar(h2[t][:, lo:hi], h2_sums(t, lo, hi), SIXTEENTH, None, ALU.mult)
+                else:
+                    nc.scalar.activation(h2[t][:, lo:hi], h2_sums(t, lo, hi), COPY, scale=SIXTEENTH)
 
-        st = [held.tile([P, S], F32, name="st%d" % t) for t in range(TILES)]
+        st = [held.tile([P, S + SPARE * (t != 2)], F32, name="st%d" % t) for t in range(TILES)]
+        for t in (0, 1, 3):
+            nc.gpsimd.memset(st[t][:, S:], 0.0)
 
         def larger(t):
             at4 = held.tile([P, S], F32, name="at4_%d" % t, tag="at4_%d" % t if t % 2 else "at4_vector")
-            for lo, hi in HALVES:
+            for lo, hi in ((0, S),) if t % 2 else HALVES:
                 picked = h2[t][:].indirect(entries(n4_t, lo, hi))
                 if t % 2:
                     nc.scalar.activation(at4[:, lo:hi], picked, COPY)
                 else:
                     nc.vector.tensor_copy(at4[:, lo:hi], picked)
-            nc.vector.tensor_tensor(st[t][:], h2[t][:], at4[:], ALU.max)
+            nc.vector.tensor_tensor(st[t][:, :S], h2[t][:, :S], at4[:], ALU.max)
 
         def result(t):
-            for i, (lo, hi) in enumerate(HALVES):
+            for i, (lo, hi) in enumerate(((0, 352), (352, 512)) if t == 2 else ((0, S),)):
                 at5 = held.tile([P, hi - lo], F32, name="at5_%d_%d" % (t, i))
                 nc.scalar.activation(at5[:], st[t][:].indirect(entries(n5_t, lo, hi)), COPY)
                 piece = held.tile([P, hi - lo], F32, name="piece_%d_%d" % (t, i))
                 nc.vector.scalar_tensor_tensor(piece[:], h2[t][:, lo:hi], -0.5, at5[:], ALU.mult, ALU.add)
                 nc.sync.dma_start(out[P * t : P * (t + 1), lo:hi], piece[:])
 
-        for t in (0, 1, 3, 2):
+        for t in (1, 0, 3, 2):
             larger(t)
-        for t in (0, 1, 3, 2):
+        for t in (1, 0, 3, 2):
             result(t)

@@ -88,8 +88,8 @@ def tile_picked_codetrimhopb_none_p_kernel(
         gs_bank = psum.tile([P, 4, P], F32, name="gs_bank", tag="second0")
         for t in range(4):
             nc.tensor.transpose(gs_bank[:, t, :], gs_t[:, t : t + 1].to_broadcast([P, P]), identity[:])
-        gs_row = held.tile([P, P, 4], F32, name="gs_row")
-        nc.scalar.activation(gs_row[:], gs_bank[:].rearrange("p t n -> p n t"), COPY)
+        gs_row = held.tile([P, 2, P, 2], F32, name="gs_row")
+        nc.scalar.activation(gs_row[:], gs_bank[:].rearrange("p (u e) n -> p u n e", u=2), COPY)
 
         h = []
 
@@ -124,7 +124,7 @@ def tile_picked_codetrimhopb_none_p_kernel(
         w2_codes = held.tile([P, H], U32, name="w2_codes", align_bytes=64)
         nc.vector.tensor_copy(w2_codes[:], d_table[:].indirect(k2_t[:]))
 
-        h2_banks = [psum.tile([P, S], F32, name="h2_bank%d" % t, tag="second%d" % t) for t in range(TILES)]
+        h2_banks = [psum.tile([P, S], F32, name="h2_bank%d" % t, tag="first%d" % t) for t in range(TILES)]
         later = {}
 
         def h2_sums(t, lo, hi):
@@ -135,12 +135,12 @@ def tile_picked_codetrimhopb_none_p_kernel(
         quantised = {}
 
         def finish_block(b, sums):
-            z_turned = held.tile([P, H], BF16, name="z_turned%d" % b)
-            nc.vector.tensor_tensor(z_turned[:], sums[:], gs_row[:].rearrange("p n t -> p (n t)"), ALU.mult)
-            pairs = z_turned[:].bitcast(F32)
-            back = psum.tile([P, 2, P], F32, name="back%d" % b, tag="first%d" % b)
+            z_turned = held.tile([P, 2, P, 2], BF16, name="z_turned%d" % b)
+            nc.vector.tensor_tensor(z_turned[:], sums[:].rearrange("j (n u e) -> j u n e", u=2, e=2), gs_row[:], ALU.mult)
+            pairs = z_turned[:].rearrange("j u n e -> j (u n e)").bitcast(F32)
+            back = psum.tile([P, 2, P], F32, name="back%d" % b, tag="second%d" % b)
             for u in range(2):
-                nc.tensor.transpose(back[:, u, :], pairs[:, u : H // 2 : 2], identity[:])
+                nc.tensor.transpose(back[:, u, :], pairs[:, P * u : P * (u + 1)], identity[:])
             z_grouped = held.tile([P, P, 2], F32, name="z_grouped%d" % b, align_bytes=64)
             if b in (0, 1, 2):
                 nc.scalar.copy(z_grouped[:], back[:].rearrange("p u r -> p r u"))
@@ -168,13 +168,13 @@ def tile_picked_codetrimhopb_none_p_kernel(
                     stop=True,
                 )
 
-        sums = [psum.tile([P, H], F32, name="sums%d" % b, tag="first%d" % b) for b in range(BLOCKS)]
+        sums = [psum.tile([P, H], F32, name="sums%d" % b, tag="second%d" % b) for b in range(BLOCKS)]
 
         def add_turned(b, t, term, start=False, stop=False):
             nc.tensor.matmul(sums[b][:, P * t : P * (t + 1)], term, identity[:], start=start, stop=stop, is_transpose=True)
 
-        for b in range(BLOCKS):
-            for t in range(TILES):
+        for t in range(TILES):
+            for b in range(BLOCKS):
                 add_turned(b, t, h[t][:, P * b : P * (b + 1)], start=(t == 0))
 
         for c, (lo, hi) in enumerate(CHUNKS):
@@ -196,9 +196,9 @@ def tile_picked_codetrimhopb_none_p_kernel(
         h2 = [held.tile([P, S + SPARE * (t % 2)], F32, name="h2_%d" % t, tag="window%d" % t) for t in range(TILES)]
         for t in (1, 3):
             nc.gpsimd.memset(h2[t][:, S:], 0.0)
-        scalar_bank = psum.tile([P, HALF], F32, name="later_scalar", tag="first0")
-        vector_bank = psum.tile([P, 2, HALF], F32, name="later_vector", tag="first1")
-        other_bank = psum.tile([P, HALF], F32, name="later_other", tag="first2")
+        scalar_bank = psum.tile([P, HALF], F32, name="later_scalar", tag="second0")
+        vector_bank = psum.tile([P, 2, HALF], F32, name="later_vector", tag="second1")
+        other_bank = psum.tile([P, HALF], F32, name="later_other", tag="second2")
         later[1] = scalar_bank
         later[3] = vector_bank[:, 0, :]
         later[0] = vector_bank[:, 1, :]

@@ -17,13 +17,19 @@ P = 128
 K, T, S, G, H = 512, 1024, 512, 2048, 512
 TILES = H // P
 BLOCKS = S // P
-HALF = 256
+HALF = S // 2
+HALVES = ((0, HALF), (HALF, S))
 SIXTEENTH = 0.0625
-CHUNKS = ((0, 384), (384, 512))
-HALVES = ((0, HALF), (HALF, 2 * HALF))
+PER_COLUMN = 16
+QUADRANT = 32
+BLOCK_PARTITIONS = 8
 
+STRETCHES = ((0, S - P), (S - P, S))
 ORDER = (1, 0, 3, 2)
+FIRST, LAST = ORDER[0], ORDER[-1]
+LAST_PIECES = ((0, 352), (352, S))
 SPARE = 16
+
 FLOPS = 2 * (2 * K * H * S)
 
 
@@ -33,16 +39,18 @@ def tile_picked_codetrimhopb_none_p_kernel(
     nc = tc.nc
     with ExitStack() as ctx:
         held = ctx.enter_context(tc.tile_pool(name="held", bufs=1))
-        ring = ctx.enter_context(tc.tile_pool(name="ring", bufs=2))
         psum = ctx.enter_context(tc.psum_pool(name="psum", bufs=1))
 
         def load_list(name, source):
-            tile = held.tile([P, S // 16], U16, name=name)
+            tile = held.tile([P, S // PER_COLUMN], U16, name=name)
             nc.sync.dma_start(tile[:], source)
             return tile
 
         def entries(tile, lo, hi):
-            return tile[:, lo // 16 : hi // 16]
+            return tile[:, lo // PER_COLUMN : hi // PER_COLUMN]
+
+        def group(i):
+            return slice(P * i, P * (i + 1))
 
         d_bytes = held.tile([P, G], U8, name="d_bytes")
         x_bytes = held.tile([P, T], U8, name="x_bytes")
@@ -51,190 +59,166 @@ def tile_picked_codetrimhopb_none_p_kernel(
 
         offs_t = load_list("offs_t", offs)
         k1_t = load_list("k1_t", k1)
-        nc.sync.dma_start(x_bytes[0:P:8, :].bitcast(I32), x_scales[0].bitcast(I32))
-        nc.sync.dma_start(d_bytes[0:P:8, :].bitcast(I32), d_scales[0].bitcast(I32))
+        nc.sync.dma_start(x_bytes[0:P:BLOCK_PARTITIONS, :].bitcast(I32), x_scales[0].bitcast(I32))
+        nc.sync.dma_start(d_bytes[0:P:BLOCK_PARTITIONS, :].bitcast(I32), d_scales[0].bitcast(I32))
         x_table = held.tile([P, T], U32, name="x_table")
-        nc.sync.dma_start(x_table[:].bitcast(I32), x_words[0].rearrange("p n t -> p (n t)").bitcast(I32))
+        nc.sync.dma_start(x_table[:].bitcast(I32), x_words[0].rearrange("p n r -> p (n r)").bitcast(I32))
         n3_t = load_list("n3_t", n3)
         n1_t = load_list("n1_t", n1)
         k2_t = load_list("k2_t", k2)
         d_table = held.tile([P, G], U32, name="d_table")
-        nc.sync.dma_start(d_table[:].bitcast(I32), d_words[0].rearrange("p n t -> p (n t)").bitcast(I32))
+        nc.sync.dma_start(d_table[:].bitcast(I32), d_words[0].rearrange("p n r -> p (n r)").bitcast(I32))
         n2_t = load_list("n2_t", n2)
         n4_t = load_list("n4_t", n4)
         n5_t = load_list("n5_t", n5)
         gs_t = held.tile([P, 4], F32, name="gs_t")
-        nc.gpsimd.dma_start(gs_t[:], gs.rearrange("(p t) o -> p (t o)", t=4))
+        nc.gpsimd.dma_start(gs_t[:], gs.rearrange("(p r) o -> p (r o)", r=4))
 
-        early_planes = held.tile([P, H + S], U8, name="early_planes", align_bytes=64)
+        first_planes = held.tile([P, H + S], U8, name="first_planes", align_bytes=64)
         w2_plane = held.tile([P, H], U8, name="w2_plane", align_bytes=64)
-        nc.gpsimd.memset(early_planes[:].bitcast(I32), 0)
+        nc.gpsimd.memset(first_planes[:].bitcast(I32), 0)
         nc.gpsimd.memset(w2_plane[:].bitcast(I32), 0)
         identity = held.tile([P, P], F32, name="identity")
         make_identity(nc, identity[:])
 
         def place_rows(planes, picked):
-            for q in range(4):
-                nc.sync.dma_start(planes[32 * q : 32 * q + 4, :].bitcast(I32), picked[32 * q : 32 * q + 32 : 8, :].bitcast(I32))
+            for q0 in range(0, P, QUADRANT):
+                nc.sync.dma_start(
+                    planes[q0 : q0 + 4, :].bitcast(I32),
+                    picked[q0 : q0 + QUADRANT : BLOCK_PARTITIONS, :].bitcast(I32),
+                )
 
-        early = held.tile([P, H + S], U8, name="early")
-        nc.vector.tensor_copy(early[:, H:], x_bytes[:].indirect(offs_t[:]))
-        nc.vector.tensor_copy(early[:, :H], d_bytes[:].indirect(k1_t[:]))
-        place_rows(early_planes, early)
-        x_plane = early_planes[:, H:]
+        first_picked = held.tile([P, H + S], U8, name="first_picked", tag="picked_bytes")
+        nc.vector.tensor_copy(first_picked[:, H:], x_bytes[:].indirect(offs_t[:]))
+        nc.vector.tensor_copy(first_picked[:, :H], d_bytes[:].indirect(k1_t[:]))
+        place_rows(first_planes, first_picked)
+        w1_plane, x_plane = first_planes[:, :H], first_planes[:, H:]
         x_codes = held.tile([P, S], U32, name="x_codes", align_bytes=64)
         nc.vector.tensor_copy(x_codes[:], x_table[:].indirect(offs_t[:]))
 
-        gs_bank = psum.tile([P, 4, P], F32, name="gs_bank", tag="second0")
-        for t in range(4):
-            nc.tensor.transpose(gs_bank[:, t, :], gs_t[:, t : t + 1].to_broadcast([P, P]), identity[:])
+        gs_bank = psum.tile([P, 4, P], F32, name="gs_bank", tag="turned0")
+        for r in range(4):
+            nc.tensor.transpose(gs_bank[:, r, :], gs_t[:, r : r + 1].to_broadcast([P, P]), identity[:])
         gs_row = held.tile([P, 2, P, 2], F32, name="gs_row")
         nc.scalar.activation(gs_row[:], gs_bank[:].rearrange("p (u e) n -> p u n e", u=2), COPY)
 
+        def leave_bank(on_scalar, rows, bank):
+            if on_scalar:
+                nc.scalar.activation(rows, bank, COPY, scale=SIXTEENTH)
+            else:
+                nc.vector.tensor_scalar(rows, bank, SIXTEENTH, None, ALU.mult)
+
         h = []
+        for i, (lo, hi) in enumerate(HALVES):
+            w1_codes = held.tile([P, HALF], U32, name="w1_codes%d" % i, align_bytes=64)
+            nc.vector.tensor_copy(w1_codes[:], d_table[:].indirect(entries(k1_t, lo, hi)))
+            for t in range(lo // P, hi // P):
+                rows = held.tile([P, S], F32, name="h%d" % t, tag="window%d" % t)
+                for c0, c1 in HALVES if t == 0 else ((0, S),):
+                    bank = psum.tile([P, c1 - c0], F32, name="h_bank%d_%d" % (t, c0), tag="rows%d" % (TILES - 1 if c0 else t))
+                    nc.tensor.matmul_mx(
+                        out=bank[:],
+                        lhsT=w1_codes[:, group(t - lo // P)].bitcast(FP8X4),
+                        lhsT_scale=w1_plane[:, group(t)],
+                        rhs=x_codes[:, c0:c1].bitcast(FP8X4),
+                        rhs_scale=x_plane[:, c0:c1],
+                        start=True,
+                        stop=True,
+                    )
+                    leave_bank(t == 0, rows[:, c0:c1], bank[:])
+                h.append(rows)
 
-        def first_product(i):
-            lo, hi = HALVES[i]
-            codes = held.tile([P, HALF], U32, name="w1_codes%d" % i, align_bytes=64)
-            nc.vector.tensor_copy(codes[:], d_table[:].indirect(entries(k1_t, lo, hi)))
-            for t in (2 * i, 2 * i + 1):
-                cols = slice(P * t - lo, P * (t + 1) - lo)
-                bank = psum.tile([P, S], F32, name="h_bank%d" % t, tag="first%d" % t)
-                nc.tensor.matmul_mx(
-                    out=bank[:],
-                    lhsT=codes[:, cols].bitcast(FP8X4),
-                    lhsT_scale=early_planes[:, P * t : P * (t + 1)],
-                    rhs=x_codes[:].bitcast(FP8X4),
-                    rhs_scale=x_plane,
-                    start=True,
-                    stop=True,
-                )
-                row = held.tile([P, S], F32, name="h%d" % t, tag="window%d" % t)
-                if t in (2, 3):
-                    nc.vector.tensor_scalar(row[:], bank[:], SIXTEENTH, None, ALU.mult)
-                else:
-                    nc.scalar.activation(row[:], bank[:], COPY, scale=SIXTEENTH)
-                h.append(row)
-
-        first_product(0)
-        first_product(1)
-        late = held.tile([P, H], U8, name="late", tag="early")
-        nc.vector.tensor_copy(late[:], d_bytes[:].indirect(k2_t[:]))
-        place_rows(w2_plane, late)
+        w2_picked = held.tile([P, H], U8, name="w2_picked", tag="picked_bytes")
+        nc.vector.tensor_copy(w2_picked[:], d_bytes[:].indirect(k2_t[:]))
+        place_rows(w2_plane, w2_picked)
         w2_codes = held.tile([P, H], U32, name="w2_codes", align_bytes=64)
         nc.vector.tensor_copy(w2_codes[:], d_table[:].indirect(k2_t[:]))
 
-        h2_banks = [psum.tile([P, S], F32, name="h2_bank%d" % t, tag="first%d" % t) for t in range(TILES)]
-        later = {}
+        sums = [psum.tile([P, H], F32, name="sums%d" % b, tag="turned%d" % b) for b in range(BLOCKS)]
 
-        def h2_sums(t, lo, hi):
-            if lo < HALF:
-                return h2_banks[t][:, lo:hi]
-            return later[t][:, lo - HALF : hi - HALF]
+        def add_turned(b, t, term, start=False, stop=False):
+            nc.tensor.matmul(sums[b][:, group(t)], term, identity[:], start=start, stop=stop, is_transpose=True)
 
-        quantised = {}
+        for t in range(TILES):
+            for b in range(BLOCKS):
+                add_turned(b, t, h[t][:, group(b)], start=(t == 0))
 
-        def finish_block(b, sums):
+        for lo, hi in STRETCHES:
+            for t in range(TILES):
+                at1 = held.tile([P, hi - lo], F32, name="at1_%d_%d" % (lo, t))
+                at2 = held.tile([P, hi - lo], F32, name="at2_%d_%d" % (lo, t))
+                minus3 = held.tile([P, hi - lo], F32, name="minus3_%d_%d" % (lo, t))
+                least = held.tile([P, hi - lo], F32, name="least_%d_%d" % (lo, t))
+                nc.scalar.activation(minus3[:], h[t][:].indirect(entries(n3_t, lo, hi)), COPY, scale=-1.0)
+                nc.scalar.activation(at1[:], h[t][:].indirect(entries(n1_t, lo, hi)), COPY)
+                nc.vector.tensor_copy(at2[:], h[t][:].indirect(entries(n2_t, lo, hi)))
+                nc.vector.scalar_tensor_tensor(least[:], at2[:], -1.0, minus3[:], ALU.mult, ALU.min)
+                for b in range(lo // P, hi // P):
+                    add_turned(b, t, at1[:, group(b - lo // P)])
+                    add_turned(b, t, least[:, group(b - lo // P)], stop=(t == TILES - 1))
+
+        z = []
+        for b in range(BLOCKS):
             z_turned = held.tile([P, 2, P, 2], BF16, name="z_turned%d" % b)
-            nc.vector.tensor_tensor(z_turned[:], sums[:].rearrange("j (n u e) -> j u n e", u=2, e=2), gs_row[:], ALU.mult)
+            nc.vector.tensor_tensor(z_turned[:], sums[b][:].rearrange("j (n u e) -> j u n e", u=2, e=2), gs_row[:], ALU.mult)
             pairs = z_turned[:].rearrange("j u n e -> j (u n e)").bitcast(F32)
-            back = psum.tile([P, 2, P], F32, name="back%d" % b, tag="second%d" % b)
+            back = psum.tile([P, 2, P], F32, name="back%d" % b, tag="turned%d" % b)
             for u in range(2):
-                nc.tensor.transpose(back[:, u, :], pairs[:, P * u : P * (u + 1)], identity[:])
+                nc.tensor.transpose(back[:, u, :], pairs[:, group(u)], identity[:])
             z_grouped = held.tile([P, P, 2], F32, name="z_grouped%d" % b, align_bytes=64)
-            if b in (0, 1, 2):
-                nc.scalar.copy(z_grouped[:], back[:].rearrange("p u r -> p r u"))
+            if b < BLOCKS - 1:
+                nc.scalar.copy(z_grouped[:], back[:].rearrange("n u j -> n j u"))
             else:
-                nc.vector.tensor_copy(z_grouped[:], back[:].rearrange("p u r -> p r u"))
+                nc.vector.tensor_copy(z_grouped[:], back[:].rearrange("n u j -> n j u"))
             z_codes = held.tile([P, P], U32, name="z_codes%d" % b, align_bytes=64)
             z_plane = held.tile([P, P], U8, name="z_plane%d" % b, align_bytes=64)
             nc.vector.quantize_mx(
                 out=z_codes[:].bitcast(FP8X4),
                 scales=z_plane[:],
-                in_=z_grouped[:].rearrange("p r u -> p (r u)").bitcast(BF16),
+                in_=z_grouped[:].rearrange("n j u -> n (j u)").bitcast(BF16),
             )
-            quantised[b] = (z_codes, z_plane)
+            z.append((z_codes, z_plane))
 
-        def second_product(b):
-            z_codes, z_plane = quantised[b]
-            for t in ORDER:
-                nc.tensor.matmul_mx(
-                    out=h2_sums(t, P * b, P * (b + 1)),
-                    lhsT=w2_codes[:, P * t : P * (t + 1)].bitcast(FP8X4),
-                    lhsT_scale=w2_plane[:, P * t : P * (t + 1)],
-                    rhs=z_codes[:].bitcast(FP8X4),
-                    rhs_scale=z_plane[:],
-                    start=True,
-                    stop=True,
-                )
-
-        sums = [psum.tile([P, H], F32, name="sums%d" % b, tag="second%d" % b) for b in range(BLOCKS)]
-
-        def add_turned(b, t, term, start=False, stop=False):
-            nc.tensor.matmul(sums[b][:, P * t : P * (t + 1)], term, identity[:], start=start, stop=stop, is_transpose=True)
-
-        for t in range(TILES):
-            for b in range(BLOCKS):
-                add_turned(b, t, h[t][:, P * b : P * (b + 1)], start=(t == 0))
-
-        for c, (lo, hi) in enumerate(CHUNKS):
-            blocks = range(lo // P, hi // P)
-            for t in range(TILES):
-                at1 = held.tile([P, hi - lo], F32, name="at1_%d_%d" % (c, t))
-                at2 = ring.tile([P, hi - lo], F32, name="at2_%d_%d" % (c, t), tag="at2")
-                minus3 = held.tile([P, hi - lo], F32, name="minus3_%d_%d" % (c, t))
-                least = held.tile([P, hi - lo], F32, name="least_%d_%d" % (c, t))
-                nc.scalar.activation(minus3[:], h[t][:].indirect(entries(n3_t, lo, hi)), COPY, scale=-1.0)
-                nc.scalar.activation(at1[:], h[t][:].indirect(entries(n1_t, lo, hi)), COPY)
-                nc.vector.tensor_copy(at2[:], h[t][:].indirect(entries(n2_t, lo, hi)))
-                nc.vector.scalar_tensor_tensor(least[:], at2[:], -1.0, minus3[:], ALU.mult, ALU.min)
-                for b in blocks:
-                    add_turned(b, t, at1[:, P * b - lo : P * (b + 1) - lo])
-                    add_turned(b, t, least[:, P * b - lo : P * (b + 1) - lo], stop=(t == TILES - 1))
-        for b in range(BLOCKS):
-            finish_block(b, sums[b])
         h2 = [held.tile([P, S + SPARE * (t % 2)], F32, name="h2_%d" % t, tag="window%d" % t) for t in range(TILES)]
-        for t in (1, 3):
+        for t in range(1, TILES, 2):
             nc.gpsimd.memset(h2[t][:, S:], 0.0)
-        scalar_bank = psum.tile([P, HALF], F32, name="later_scalar", tag="second0")
-        vector_bank = psum.tile([P, 2, HALF], F32, name="later_vector", tag="second1")
-        other_bank = psum.tile([P, HALF], F32, name="later_other", tag="second2")
-        later[1] = scalar_bank
-        later[3] = vector_bank[:, 0, :]
-        later[0] = vector_bank[:, 1, :]
-        later[2] = other_bank
-        for lo, hi in HALVES:
+        early_banks = {t: psum.tile([P, HALF], F32, name="early_bank%d" % t, tag="rows%d" % t) for t in range(TILES)}
+        first_bank = psum.tile([P, HALF], F32, name="first_bank", tag="turned0")
+        middle_bank = psum.tile([P, 2, HALF], F32, name="middle_bank", tag="turned1")
+        last_bank = psum.tile([P, HALF], F32, name="last_bank", tag="turned2")
+        late_banks = {FIRST: first_bank, ORDER[2]: middle_bank[:, 0, :], ORDER[1]: middle_bank[:, 1, :], LAST: last_bank}
+        for (lo, hi), banks in zip(HALVES, (early_banks, late_banks)):
             for b in range(lo // P, hi // P):
-                second_product(b)
+                z_codes, z_plane = z[b]
+                for t in ORDER:
+                    nc.tensor.matmul_mx(
+                        out=banks[t][:, group(b - lo // P)],
+                        lhsT=w2_codes[:, group(t)].bitcast(FP8X4),
+                        lhsT_scale=w2_plane[:, group(t)],
+                        rhs=z_codes[:].bitcast(FP8X4),
+                        rhs_scale=z_plane[:],
+                        start=True,
+                        stop=True,
+                    )
             for t in ORDER:
-                if hi == S and t != 1:
-                    nc.vector.tensor_scalar(h2[t][:, lo:hi], h2_sums(t, lo, hi), SIXTEENTH, None, ALU.mult)
-                else:
-                    nc.scalar.activation(h2[t][:, lo:hi], h2_sums(t, lo, hi), COPY, scale=SIXTEENTH)
+                leave_bank(lo == 0 or t == FIRST, h2[t][:, lo:hi], banks[t][:, :])
 
-        st = [held.tile([P, S + SPARE * (t != 2)], F32, name="st%d" % t) for t in range(TILES)]
-        for t in (0, 1, 3):
+        st = [held.tile([P, S + SPARE * (t != LAST)], F32, name="st%d" % t) for t in range(TILES)]
+        for t in sorted(ORDER[:-1]):
             nc.gpsimd.memset(st[t][:, S:], 0.0)
-
-        def larger(t):
-            at4 = held.tile([P, S], F32, name="at4_%d" % t, tag="at4_%d" % t if t % 2 else "at4_vector")
-            for lo, hi in ((0, S),) if t % 2 else HALVES:
-                picked = h2[t][:].indirect(entries(n4_t, lo, hi))
-                if t % 2:
-                    nc.scalar.activation(at4[:, lo:hi], picked, COPY)
-                else:
-                    nc.vector.tensor_copy(at4[:, lo:hi], picked)
+        for t in ORDER:
+            if t % 2:
+                at4 = held.tile([P, S], F32, name="at4_%d" % t)
+                nc.scalar.activation(at4[:], h2[t][:].indirect(n4_t[:]), COPY)
+            else:
+                at4 = held.tile([P, S], F32, name="at4_%d" % t, tag="at4_vector")
+                for lo, hi in HALVES:
+                    nc.vector.tensor_copy(at4[:, lo:hi], h2[t][:].indirect(entries(n4_t, lo, hi)))
             nc.vector.tensor_tensor(st[t][:, :S], h2[t][:, :S], at4[:], ALU.max)
-
-        def result(t):
-            for i, (lo, hi) in enumerate(((0, 352), (352, 512)) if t == 2 else ((0, S),)):
-                at5 = held.tile([P, hi - lo], F32, name="at5_%d_%d" % (t, i))
+        for t in ORDER:
+            for lo, hi in LAST_PIECES if t == LAST else ((0, S),):
+                at5 = held.tile([P, hi - lo], F32, name="at5_%d_%d" % (t, lo))
                 nc.scalar.activation(at5[:], st[t][:].indirect(entries(n5_t, lo, hi)), COPY)
-                piece = held.tile([P, hi - lo], F32, name="piece_%d_%d" % (t, i))
+                piece = held.tile([P, hi - lo], F32, name="piece_%d_%d" % (t, lo))
                 nc.vector.scalar_tensor_tensor(piece[:], h2[t][:, lo:hi], -0.5, at5[:], ALU.mult, ALU.add)
-                nc.sync.dma_start(out[P * t : P * (t + 1), lo:hi], piece[:])
-
-        for t in (1, 0, 3, 2):
-            larger(t)
-        for t in (1, 0, 3, 2):
-            result(t)
+                nc.sync.dma_start(out[group(t), lo:hi], piece[:])

from contextlib import ExitStack

import concourse.mybir as mybir
from concourse.masks import make_identity

F32 = mybir.dt.float32
BF16 = mybir.dt.bfloat16
I32 = mybir.dt.int32
U32 = mybir.dt.uint32
U16 = mybir.dt.uint16
U8 = mybir.dt.uint8
FP8X4 = mybir.dt.float8_e4m3fn_x4
ALU = mybir.AluOpType
COPY = mybir.ActivationFunctionType.Copy

P = 128
K, T, S, G, H = 512, 1024, 512, 2048, 512
TILES = H // P
BLOCKS = S // P
HALF = S // 2
HALVES = ((0, HALF), (HALF, S))
SIXTEENTH = 0.0625
PER_COLUMN = 16
QUADRANT = 32
BLOCK_PARTITIONS = 8

STRETCHES = ((0, S - P), (S - P, S))
ORDER = (1, 0, 3, 2)
FIRST, LAST = ORDER[0], ORDER[-1]
LAST_PIECES = ((0, 352), (352, S))
SPARE = 16

FLOPS = 2 * (2 * K * H * S)


def tile_picked_codetrimhopb_none_p_kernel(
    tc, x_words, x_scales, d_words, d_scales, gs, offs, k1, n1, n2, n3, k2, n4, n5, out
):
    nc = tc.nc
    with ExitStack() as ctx:
        held = ctx.enter_context(tc.tile_pool(name="held", bufs=1))
        psum = ctx.enter_context(tc.psum_pool(name="psum", bufs=1))

        def load_list(name, source):
            tile = held.tile([P, S // PER_COLUMN], U16, name=name)
            nc.sync.dma_start(tile[:], source)
            return tile

        def entries(tile, lo, hi):
            return tile[:, lo // PER_COLUMN : hi // PER_COLUMN]

        def group(i):
            return slice(P * i, P * (i + 1))

        d_bytes = held.tile([P, G], U8, name="d_bytes")
        x_bytes = held.tile([P, T], U8, name="x_bytes")
        nc.vector.memset(x_bytes[:].bitcast(I32), 0)
        nc.vector.memset(d_bytes[:].bitcast(I32), 0)

        offs_t = load_list("offs_t", offs)
        k1_t = load_list("k1_t", k1)
        nc.sync.dma_start(x_bytes[0:P:BLOCK_PARTITIONS, :].bitcast(I32), x_scales[0].bitcast(I32))
        nc.sync.dma_start(d_bytes[0:P:BLOCK_PARTITIONS, :].bitcast(I32), d_scales[0].bitcast(I32))
        x_table = held.tile([P, T], U32, name="x_table")
        nc.sync.dma_start(x_table[:].bitcast(I32), x_words[0].rearrange("p n r -> p (n r)").bitcast(I32))
        n3_t = load_list("n3_t", n3)
        n1_t = load_list("n1_t", n1)
        k2_t = load_list("k2_t", k2)
        d_table = held.tile([P, G], U32, name="d_table")
        nc.sync.dma_start(d_table[:].bitcast(I32), d_words[0].rearrange("p n r -> p (n r)").bitcast(I32))
        n2_t = load_list("n2_t", n2)
        n4_t = load_list("n4_t", n4)
        n5_t = load_list("n5_t", n5)
        gs_t = held.tile([P, 4], F32, name="gs_t")
        nc.gpsimd.dma_start(gs_t[:], gs.rearrange("(p r) o -> p (r o)", r=4))

        first_planes = held.tile([P, H + S], U8, name="first_planes", align_bytes=64)
        w2_plane = held.tile([P, H], U8, name="w2_plane", align_bytes=64)
        nc.gpsimd.memset(first_planes[:].bitcast(I32), 0)
        nc.gpsimd.memset(w2_plane[:].bitcast(I32), 0)
        identity = held.tile([P, P], F32, name="identity")
        make_identity(nc, identity[:])

        def place_rows(planes, picked):
            for q0 in range(0, P, QUADRANT):
                nc.sync.dma_start(
                    planes[q0 : q0 + 4, :].bitcast(I32),
                    picked[q0 : q0 + QUADRANT : BLOCK_PARTITIONS, :].bitcast(I32),
                )

        first_picked = held.tile([P, H + S], U8, name="first_picked", tag="picked_bytes")
        nc.vector.tensor_copy(first_picked[:, H:], x_bytes[:].indirect(offs_t[:]))
        nc.vector.tensor_copy(first_picked[:, :H], d_bytes[:].indirect(k1_t[:]))
        place_rows(first_planes, first_picked)
        w1_plane, x_plane = first_planes[:, :H], first_planes[:, H:]
        x_codes = held.tile([P, S], U32, name="x_codes", align_bytes=64)
        nc.vector.tensor_copy(x_codes[:], x_table[:].indirect(offs_t[:]))

        gs_bank = psum.tile([P, 4, P], F32, name="gs_bank", tag="turned0")
        for r in range(4):
            nc.tensor.transpose(gs_bank[:, r, :], gs_t[:, r : r + 1].to_broadcast([P, P]), identity[:])
        gs_row = held.tile([P, 2, P, 2], F32, name="gs_row")
        nc.scalar.activation(gs_row[:], gs_bank[:].rearrange("p (u e) n -> p u n e", u=2), COPY)

        def leave_bank(on_scalar, rows, bank):
            if on_scalar:
                nc.scalar.activation(rows, bank, COPY, scale=SIXTEENTH)
            else:
                nc.vector.tensor_scalar(rows, bank, SIXTEENTH, None, ALU.mult)

        h = []
        for i, (lo, hi) in enumerate(HALVES):
            w1_codes = held.tile([P, HALF], U32, name="w1_codes%d" % i, align_bytes=64)
            nc.vector.tensor_copy(w1_codes[:], d_table[:].indirect(entries(k1_t, lo, hi)))
            for t in range(lo // P, hi // P):
                rows = held.tile([P, S], F32, name="h%d" % t, tag="window%d" % t)
                for c0, c1 in HALVES if t == 0 else ((0, S),):
                    bank = psum.tile([P, c1 - c0], F32, name="h_bank%d_%d" % (t, c0), tag="rows%d" % (TILES - 1 if c0 else t))
                    nc.tensor.matmul_mx(
                        out=bank[:],
                        lhsT=w1_codes[:, group(t - lo // P)].bitcast(FP8X4),
                        lhsT_scale=w1_plane[:, group(t)],
                        rhs=x_codes[:, c0:c1].bitcast(FP8X4),
                        rhs_scale=x_plane[:, c0:c1],
                        start=True,
                        stop=True,
                    )
                    leave_bank(t == 0, rows[:, c0:c1], bank[:])
                h.append(rows)

        w2_picked = held.tile([P, H], U8, name="w2_picked", tag="picked_bytes")
        nc.vector.tensor_copy(w2_picked[:], d_bytes[:].indirect(k2_t[:]))
        place_rows(w2_plane, w2_picked)
        w2_codes = held.tile([P, H], U32, name="w2_codes", align_bytes=64)
        nc.vector.tensor_copy(w2_codes[:], d_table[:].indirect(k2_t[:]))

        sums = [psum.tile([P, H], F32, name="sums%d" % b, tag="turned%d" % b) for b in range(BLOCKS)]

        def add_turned(b, t, term, start=False, stop=False):
            nc.tensor.matmul(sums[b][:, group(t)], term, identity[:], start=start, stop=stop, is_transpose=True)

        for t in range(TILES):
            for b in range(BLOCKS):
                add_turned(b, t, h[t][:, group(b)], start=(t == 0))

        for lo, hi in STRETCHES:
            for t in range(TILES):
                at1 = held.tile([P, hi - lo], F32, name="at1_%d_%d" % (lo, t))
                at2 = held.tile([P, hi - lo], F32, name="at2_%d_%d" % (lo, t))
                minus3 = held.tile([P, hi - lo], F32, name="minus3_%d_%d" % (lo, t))
                least = held.tile([P, hi - lo], F32, name="least_%d_%d" % (lo, t))
                nc.scalar.activation(minus3[:], h[t][:].indirect(entries(n3_t, lo, hi)), COPY, scale=-1.0)
                nc.scalar.activation(at1[:], h[t][:].indirect(entries(n1_t, lo, hi)), COPY)
                nc.vector.tensor_copy(at2[:], h[t][:].indirect(entries(n2_t, lo, hi)))
                nc.vector.scalar_tensor_tensor(least[:], at2[:], -1.0, minus3[:], ALU.mult, ALU.min)
                for b in range(lo // P, hi // P):
                    add_turned(b, t, at1[:, group(b - lo // P)])
                    add_turned(b, t, least[:, group(b - lo // P)], stop=(t == TILES - 1))

        z = []
        for b in range(BLOCKS):
            z_turned = held.tile([P, 2, P, 2], BF16, name="z_turned%d" % b)
            nc.vector.tensor_tensor(z_turned[:], sums[b][:].rearrange("j (n u e) -> j u n e", u=2, e=2), gs_row[:], ALU.mult)
            pairs = z_turned[:].rearrange("j u n e -> j (u n e)").bitcast(F32)
            back = psum.tile([P, 2, P], F32, name="back%d" % b, tag="turned%d" % b)
            for u in range(2):
                nc.tensor.transpose(back[:, u, :], pairs[:, group(u)], identity[:])
            z_grouped = held.tile([P, P, 2], F32, name="z_grouped%d" % b, align_bytes=64)
            if b < BLOCKS - 1:
                nc.scalar.copy(z_grouped[:], back[:].rearrange("n u j -> n j u"))
            else:
                nc.vector.tensor_copy(z_grouped[:], back[:].rearrange("n u j -> n j u"))
            z_codes = held.tile([P, P], U32, name="z_codes%d" % b, align_bytes=64)
            z_plane = held.tile([P, P], U8, name="z_plane%d" % b, align_bytes=64)
            nc.vector.quantize_mx(
                out=z_codes[:].bitcast(FP8X4),
                scales=z_plane[:],
                in_=z_grouped[:].rearrange("n j u -> n (j u)").bitcast(BF16),
            )
            z.append((z_codes, z_plane))

        h2 = [held.tile([P, S + SPARE * (t % 2)], F32, name="h2_%d" % t, tag="window%d" % t) for t in range(TILES)]
        for t in range(1, TILES, 2):
            nc.gpsimd.memset(h2[t][:, S:], 0.0)
        early_banks = {t: psum.tile([P, HALF], F32, name="early_bank%d" % t, tag="rows%d" % t) for t in range(TILES)}
        first_bank = psum.tile([P, HALF], F32, name="first_bank", tag="turned0")
        middle_bank = psum.tile([P, 2, HALF], F32, name="middle_bank", tag="turned1")
        last_bank = psum.tile([P, HALF], F32, name="last_bank", tag="turned2")
        late_banks = {FIRST: first_bank, ORDER[2]: middle_bank[:, 0, :], ORDER[1]: middle_bank[:, 1, :], LAST: last_bank}
        for (lo, hi), banks in zip(HALVES, (early_banks, late_banks)):
            for b in range(lo // P, hi // P):
                z_codes, z_plane = z[b]
                for t in ORDER:
                    nc.tensor.matmul_mx(
                        out=banks[t][:, group(b - lo // P)],
                        lhsT=w2_codes[:, group(t)].bitcast(FP8X4),
                        lhsT_scale=w2_plane[:, group(t)],
                        rhs=z_codes[:].bitcast(FP8X4),
                        rhs_scale=z_plane[:],
                        start=True,
                        stop=True,
                    )
            for t in ORDER:
                leave_bank(lo == 0 or t == FIRST, h2[t][:, lo:hi], banks[t][:, :])

        st = [held.tile([P, S + SPARE * (t != LAST)], F32, name="st%d" % t) for t in range(TILES)]
        for t in sorted(ORDER[:-1]):
            nc.gpsimd.memset(st[t][:, S:], 0.0)
        for t in ORDER:
            if t % 2:
                at4 = held.tile([P, S], F32, name="at4_%d" % t)
                nc.scalar.activation(at4[:], h2[t][:].indirect(n4_t[:]), COPY)
            else:
                at4 = held.tile([P, S], F32, name="at4_%d" % t, tag="at4_vector")
                for lo, hi in HALVES:
                    nc.vector.tensor_copy(at4[:, lo:hi], h2[t][:].indirect(entries(n4_t, lo, hi)))
            nc.vector.tensor_tensor(st[t][:, :S], h2[t][:, :S], at4[:], ALU.max)
        for t in ORDER:
            for lo, hi in LAST_PIECES if t == LAST else ((0, S),):
                at5 = held.tile([P, hi - lo], F32, name="at5_%d_%d" % (t, lo))
                nc.scalar.activation(at5[:], st[t][:].indirect(entries(n5_t, lo, hi)), COPY)
                piece = held.tile([P, hi - lo], F32, name="piece_%d_%d" % (t, lo))
                nc.vector.scalar_tensor_tensor(piece[:], h2[t][:, lo:hi], -0.5, at5[:], ALU.mult, ALU.add)
                nc.sync.dma_start(out[group(t), lo:hi], piece[:])
